import numpy as np, ml_dtypes
CORES = [113,118,241,246]
N = 4
BF = ml_dtypes.bfloat16
def f(rng, *shape):
    return (rng.standard_normal(shape, dtype=np.float32) * np.exp2(rng.integers(-2, 3, shape[:-1] + (1,)))).astype(BF)
def wide(rng, *shape):
    v = f(rng, *shape).astype(np.float32); k = shape[:-2] + (1, shape[-1])
    return (v * np.exp2(rng.integers(-6, 7, k)) * (rng.random(k) > 0.0625)).astype(BF)
M, K, TR, CAP = 2048, 48, 3, 288
D = 16 * K
def hashes(s, n):
    lo = ((s & 4095) + 1597 * n) & 4095; b = ((s >> 12) + ((lo * lo) >> 6)) & 4095
    return (lo + ((b * b) >> 6)) & 4095, b
def seed_of(a, b, n):
    lo = (a - ((b * b) >> 6)) & 4095
    return ((b - ((lo * lo) >> 6)) & 4095) * 4096 + ((lo - 1597 * n) & 4095)
def owners(t, s):
    a, b = hashes(np.asarray(s, np.int64)[..., None], (TR + 1) * np.arange(K)); w = (a * N) >> 12
    return np.where(b < t[w], w, t[N + w]).astype(np.int64)
def loads(t, s):
    o = owners(t, s); return np.stack([np.sum(o == q, -1) for q in range(N)], -1)
def sixteen(rng, t, keep=()):
    m = 16 - len(keep); kept = np.array(keep, np.int64); base = np.sum(loads(t, kept), 0)
    pool = rng.integers(0, 1 << 24, 1024); c = loads(t, pool); ok = np.flatnonzero(np.all(c * m <= CAP - base, 1)); j = np.arange(m)
    for u in range(m):
        if np.all(np.sum(c[j], 0) + base <= CAP): break
        j[u] = rng.choice(ok)
    return rng.permutation(np.concatenate([pool[j], kept]))
def ranks(rng, least):
    return np.concatenate([rng.integers(least, 4097, N), rng.permutation(N)]).astype(np.int64)
def absent(rng):
    w = rng.permutation(N); t = np.zeros(2 * N, np.int64)
    t[w] = (8192 * np.arange(N) + N - 1) // (2 * (N - 1)); t[N + w] = np.roll(w, -1); return t
def history(rng, dens):
    w = np.zeros((N, 128, M), np.float32)
    for q in range(N):
        for r in range(N):
            w[q] += np.float32(2 ** r) * (rng.random((128, M), dtype=np.float32) < dens[r][:, None])
    return w.astype(BF)
def seeds(rng, rk):
    return np.stack([np.stack([sixteen(rng, rk[g]) for g in range(8)]) for r in range(N)])
def complete(rng, rk, sd, dens=None):
    if dens is None: dens = rng.choice(np.array([0.1, 0.5, 0.9]), (N, 128))
    return {"sd": np.reshape(sd, (N, 128, 1)).astype(np.int32), "rk": np.stack([rk] * N).astype(np.int32), "thr": rng.integers(0, 4097, (N, 8, M)).astype(np.int32),
            "ali": rng.integers(0, M, (N, 8, M)).astype(np.int32), "seen": history(rng, dens), "vec": f(rng, N, 128, M)}
def setup_inputs(rng):
    rk = np.stack([ranks(rng, 2800) for g in range(8)]); return complete(rng, rk, seeds(rng, rk))
def setup_inputs_full(rng):
    o0 = rng.integers(0, N); rk = []
    for g in range(8):
        o = (o0 + g) % N; t = np.concatenate([rng.integers(3577 - 40, 3577 + 41, N), np.full(N, o)]).astype(np.int64); t[o] = 4096; rk.append(t)
    rk = np.stack(rk); sd = seeds(rng, rk); C = CAP // 16
    far = rng.integers(0, N, 8); h = rng.permutation(8); far[h[0]] = 0; far[h[1]] = rng.integers(1, N)
    for g in range(8):
        o = (o0 + g) % N; r = (o + far[g]) % N
        pool = rng.integers(0, 1 << 24, 4096); c = loads(rk[g], pool); fine = np.all(np.delete(c, o, 1) <= C, 1); s = []
        for i in range(8):
            x = rng.integers(-2, 3)
            for v in (C + x, C - x): s.append(pool[rng.choice(np.flatnonzero(fine & (c[:, o] == v)))])
        sd[r, g] = rng.permutation(np.array(s))
    return complete(rng, rk, sd)
def setup_inputs_edges(rng):
    rk, tie = [], []
    for g in range(8):
        t = ranks(rng, 3500); w = rng.permutation(N)[:4]; t[w[0]] = 0; t[N + w[0]] = w[1]; t[w[1]] = 0; t[N + w[1]] = w[0]; t[w[2]] = rng.integers(3500, 4096); t[N + w[2]] = w[0]; t[w[3]] = 4096; rk.append(t)
        tie.append(seed_of(int(w[2]) * (4096 // N) + int(rng.integers(0, 4096 // N)), int(t[w[2]]), (TR + 1) * int(rng.integers(0, K))))
    rk = np.stack(rk); sd = np.stack([np.stack([sixteen(rng, rk[g], (0, (1 << 24) - 1, tie[g])) for g in range(8)]) for r in range(N)])
    d = complete(rng, rk, sd); z = rng.integers(0, 4, (N, 8, M)); thr = np.where(z == 0, 0, np.where(z == 1, 4096, d["thr"])); z = rng.integers(0, 4, (N, 8, M))
    ali = np.where(z == 0, 0, np.where(z == 1, M - 1, np.where(z == 2, np.arange(M), d["ali"])))
    for r in range(N):
        for g in range(8):
            q = owners(rk[g], sd[r, g])[:, ::4]; a, b = hashes(sd[r, g][:, None], ((TR + 1) * np.arange(K) + 1)[None, ::4]); e = (a * M) >> 12
            thr[q, g, e] = b; ali[q, g, e] = M - 1 - e
    d["thr"] = thr.astype(np.int32); d["ali"] = ali.astype(np.int32); return d
def setup_inputs_hot(rng):
    rk = np.stack([ranks(rng, 2800) for g in range(8)]); sd = seeds(rng, rk)
    for g in range(8):
        pool = rng.integers(0, 1 << 24, 1024); sd[rng.integers(0, N), g] = pool[rng.choice(np.flatnonzero(np.all(loads(rk[g], pool) <= CAP // 16, 1)))]
    d = complete(rng, rk, sd); h = rng.integers(0, M, (N, 8, 1)); h[:, 0] = 0; h[:, 7] = M - 1
    d["thr"] = rng.integers(0, 512, (N, 8, M)).astype(np.int32); d["ali"] = (h + np.zeros((1, 1, M), np.int64)).astype(np.int32); return d
def setup_inputs_avid(rng):
    rk = np.stack([absent(rng) for g in range(8)]); dens = rng.choice(np.array([0, 0.97, 1.0]), (N, 128)); dens[rng.integers(0, N)] = 1
    return complete(rng, rk, seeds(rng, rk), dens)
def setup_inputs_spread(rng):
    d = setup_inputs(rng); d["vec"] = wide(rng, N, 128, M); d["thr"] = (4096 >> rng.integers(0, 14, (N, 8, M))).astype(np.int32); return d
def check_inputs(d):
    bad = []
    try:
        sd, rk = d["sd"].astype(np.int64), d["rk"].astype(np.int64); w = d["seen"].astype(np.float32)
        if not ((sd >= 0) & (sd < 1 << 24)).all(): bad.append("seed")
        if not (rk == rk[:1]).all(): bad.append("rk alike on all ranks")
        if not ((rk[..., :N] >= 0) & (rk[..., :N] <= 4096) & (rk[..., N:] >= 0) & (rk[..., N:] < N)).all(): bad.append("rk")
        if not ((d["thr"] >= 0) & (d["thr"] <= 4096)).all(): bad.append("thr")
        if not ((d["ali"] >= 0) & (d["ali"] < M)).all(): bad.append("ali")
        if not ((w >= 0) & (w < 2 ** N) & (w == np.floor(w))).all(): bad.append("seen")
        if not np.isfinite(d["vec"].astype(np.float32)).all(): bad.append("finite")
        if not bad and any((np.sum(loads(rk[r, g], sd[r, 16 * g:16 * g + 16, 0]), 0) > CAP).any() for r in range(N) for g in range(8)): bad.append("cap")
    except Exception:
        bad.append("unreadable")
    return bad
def reference(sd, rk, thr, ali, seen, vec):
    chosen = np.zeros((N, 128, K), np.float32); y = np.zeros((N, 128, D), vec.dtype); n = (TR + 1) * np.arange(K); row = np.arange(16)[:, None]
    for r in range(N):
        for g in range(8):
            s = sd[r, 16 * g:16 * g + 16].astype(np.int64)
            q = owners(rk[r, g].astype(np.int64), s[:, 0])
            x = np.zeros((16, K), np.int64); done = np.zeros((16, K), bool)
            for i in range(1, TR + 1):
                a, b = hashes(s, n + i); e = (a * M) >> 12
                c = np.where(b < thr[q, g, e], e, ali[q, g, e]).astype(np.int64)
                known = (seen[q, 16 * g + row, c].astype(np.float32).astype(np.int64) >> r) & 1
                x = np.where(done, x, c); done = done | (known == 0)
            chosen[r, 16 * g:16 * g + 16] = q * M + x
            y[r, 16 * g:16 * g + 16] = vec[q.T.reshape(-1), 16 * g + row, x.T.reshape(-1)]
    return {"chosen": chosen, "y": y}

@@ -1,0 +1,260 @@
+from concourse.bass import DstId, RemoteDMATransfer
+from concourse.mybir import AluOpType as OP, ActivationFunctionType as AF
+
+M, K, N = 2048, 48, 4
+J = 16 * K
+CUTS = (0, 896, 1536, 2048)
+YV = 24
+HV = 24
+LOOKS = (((0, 48),), ((0, 48),), ((0, 24), (24, 48)))
+ORDER = {
+    "p": "pu n0 cp n1 ei cb p8",
+    "v": "TM TA PB sf ID MOD s0 tab s1 l0 si MW l1 m0 ra sg m1 E8 KZ r1 t0 r0 r2 t1 b0 b1 c0 c1 a0 a1 TS W H VV PC HH "
+         "u0 u1 u2 u3 u4 u5 u6 K0 LO o2 o1 o0 BH E16 IDN EE x00 x10 x20 M0 C0 S0 L0 P0 M1 x21 C1 F0 S1 L1 G0 hv P1 M2 C2 G1 S2 "
+         "e1 e2 F1 TK KB f1 KK f3 f2 X X16 yv",
+    "a": "d9 d14 d12 d1 d13 i6 cw d2 q0 q1 d11 d7 d0 d8 sw0 d15 sw1 k0 k1 k2 d3 d6 d4 d10 d5 h0 ha ya",
+    "t": " ".join(["pe0 po0 pe1 po1 rt"] + ["Q%d" % w for w in range(7)]
+                  + [" ".join(["y%d_%d" % (i, u) for u in range(16)] + ["Y%d" % i]) for i in range(3)] + ["z%d" % u for u in range(16)])}
+
+I4, F4, F2, H2, U2 = "int32", "float32", "bfloat16", "float16", "uint16"
+SCRATCH = {n: ("sbuf", [p, c], d) for n, p, c, d in (
+    ("PW", 128, 1024, I4), ("SW", 128, 4096, F2), ("VW", 128, 8192, F2), ("SEEN", 128, 2048, F2), ("SDI", 128, 1, I4),
+    ("RKI", 8, 8, I4), ("RKA", 8, 4, F4), ("RT", 8, 11, F4), ("TI", 128, 16, I4), ("TA", 128, 24, I4), ("T8", 128, 8, I4),
+    ("TS", 128, 8, I4), ("MI", 128, 128, F4), ("N0", 128, 192, I4), ("EI", 8, 128, F4), ("PB", 128, 1, I4),
+    ("PC", 128, 1, F4), ("K0", 128, 144, H2), ("ID", 128, 128, F2), ("ID16", 128, 128, F2), ("IDN", 128, 128, H2),
+    ("E8L", 8, 128, F4), ("MOD", 128, 16, F4), ("MW", 128, 8, F2), ("DG", 128, 2048, F2), ("SI", 128, 1, I4), ("SF", 128, 2, F4),
+    ("L0", 128, 192, I4), ("L", 128, 192, I4), ("LL", 128, 192, F4), ("TT", 128, 192, I4), ("B", 128, 192, I4),
+    ("BB", 128, 192, I4), ("AA", 128, 192, I4), ("H", 128, 144, I4), ("H16", 128, 144, U2), ("W12", 128, 48, I4),
+    ("VV", 128, 48, I4), ("TM", 128, 336, F2), ("CW", 8, 4, F4), ("CB", 8, 4, F4),
+    ("LOW8", 128, 144, I4), ("EE", 128, 144, I4), ("BH", 128, 144, H2),
+    ("S", 128, 144, I4), ("E16", 128, 144, U2), ("MK", 128, 2304, F2), ("X1", 128, 2304, H2), ("X2", 128, 1536, F2),
+    ("M1", 128, 144, I4), ("C2", 128, 144, I4), ("S2", 128, 144, I4), ("S16", 128, 96, U2), ("PAR", 128, 96, I4), ("G", 128, 144, I4),
+    ("PP", 128, 96, I4), ("TK", 128, 96, I4), ("KK", 128, 48, F4), ("KB", 128, 96, I4), ("X", 128, 48, F4), ("W", 128, 48, F4),
+    ("X16", 128, 48, U2), ("Y", 128, 768, F2))}
+SCRATCH["HP"] = ("psum", [128, 1024], F4)
+SCRATCH["HU"] = ("psum", [128, 512], F4)
+SCRATCH["DD"] = ("psum", [128, 1024], F4)
+SCRATCH["RQ"] = ("psum", [128, 512], F4)
+SCRATCH["VB"] = ("psum", [128, 512], F4)
+SEMAPHORES = ["v", "a", "t", "p", "lsd", "ltab", "lrk", "ls0", "ls1", "lvec", "pk", "sn", "vp", "s0", "s1", "fs", "x0", "x1", "x2", "fw",
+              "ls", "lf", "st"]
+
+
+def rank_program(g, core, T, topo):
+    r = T.rank_of(core)
+    if r is None:
+        return
+    others = [c for c in T.cores if c != core]
+    partner = [c for c in others if c in topo.cores_of(core)][0]
+    cross = [c for c in others if c != partner and topo.die(c) == topo.die(core)][0]
+    diag = [c for c in others if c not in (partner, cross)][0]
+    off = topo.engines(core, cross)
+    near = topo.engines(core, partner)
+    on = [e for e in near if e not in off]
+    bits = lambda es: sum(1 << e for e in es)
+    half = len(off) // 2
+    lanes = {partner: bits(on), cross: bits(off[:half]), diag: bits(off[half:])}
+    vec, act, pe = g.vector, g.scalar, g.tensor
+    eng = {"v": vec, "a": act, "t": pe, "p": g, "s": g.sync}
+    place = {name: (q, i + 1) for q in ORDER for i, name in enumerate(ORDER[q].split())}
+    todo = {}
+    lvl = {q: {} for q in eng}
+
+    def need(q, deps):
+        for d in deps:
+            s, n = place[d] if d in place else d
+            if lvl[q].get(s, 0) < n:
+                eng[q].wait_ge(T.sem[s], n)
+                lvl[q][s] = n
+
+    def call(name, deps, f, *args, **kw):
+        todo[name] = (deps, f, args, kw)
+
+    def blk(i):
+        return slice(48 * i, 48 * i + 48)
+
+    def pos(i, a=0, b=48):
+        return slice(J * i + 16 * a, J * i + 16 * b)
+
+    ts, tt, cp, copy, mm = vec.tensor_scalar, vec.tensor_tensor, vec.tensor_copy, act.activation, pe.matmul
+    SHR, AND = OP.arith_shift_right, OP.bitwise_and
+    two, last = slice(0, 96), slice(48, 192)
+    halves = (slice(0, 96), slice(96, 192))
+
+    my = slice(256 * r, 256 * r + 256)
+    g.sync.dma_start(T.SDI[:], T.sd[:]).then_inc(T.sem.lsd, 16)
+    act.dma_start(T.PW[1:128:2, my], T.ali[:]).then_inc(T.sem.ltab, 16)
+    g.sync.dma_start(T.PW[0:128:2, my], T.thr[:]).then_inc(T.sem.ltab, 16)
+    act.dma_start(T.RKI[:], T.rk[:]).then_inc(T.sem.lrk, 16)
+    for h in range(2):
+        w = slice(1024 * h, 1024 * h + 1024)
+        g.sync.dma_start(T.SEEN[:, w], T.seen[:, w]).then_inc(T.sem["ls%d" % h], 16)
+    g.sync.dma_start(T.VW[:, M * r:M * r + M], T.vec[:]).then_inc(T.sem.lvec, 16)
+
+    f = {"allow_small_or_imprecise_dtypes": True}
+
+    def ramp(*args, **kw):
+        g.iota(*args, **kw).then_inc(T.sem.p, 1)
+
+    def send(buf, a0, a1, dests):
+        tr = []
+        for d, mask, s in dests:
+            rid, pid = topo.addr(d, core)
+            tr.append(RemoteDMATransfer(dst_ids=[DstId(rid=rid, pnc=pid)], dma_engine_mask=mask, remote_sem=T.sem[s],
+                                        srcs=[T[buf][:, a0:a1]], dsts=[T[buf][:, a0:a1]]))
+        g.remote_dma_fused(tr, local_sem=T.sem.ls)
+
+    def hand(buf, a0, a1, s, es):
+        rid, pid = topo.addr(partner, core)
+        g.remote_dma(T[buf][:, a0:a1], T[buf][:, a0:a1], T.sem[s], T.sem.lf, pid, rid, bits(es))
+
+    ramp(T.TI[:, 0:16], [[-1, 16]], 0, 1)
+    ramp(T.N0[:, 0:96], [[1597, 2], [6388, 48]], -(1 << 23), 0)
+    ramp(T.MI[:], [[1, 128]], 0, -1, **f)
+    ramp(T.N0[:, 96:192], [[1597, 2], [6388, 48]], 2 * 1597 - (1 << 23), 0)
+    ramp(T.EI[:], [[16, 8], [0, 16]], 0, -16, **f)
+    ramp(T.CB[:], [[4096, 4]], 0, 0, **f)
+    far = T.rank_of(cross)
+    need("p", ["tab"])
+    send("PW", 256 * r, 256 * r + 256, [(d, lanes[d], "pk") for d in (cross, diag, partner)])
+    ramp(T.T8[:], [[-16, 8]], 0, 1)
+    for h in range(2):
+        need("p", ["sw%d" % h])
+        o = 1024 * r + 512 * h
+        send("SW", o, o + 512, [(cross, bits(off), "s%d" % h), (partner, bits(on), "sn")])
+    need("p", [("lvec", 16)])
+    pieces = list(zip(CUTS, CUTS[1:]))
+    n = len(pieces)
+    for c, (a0, a1) in enumerate(pieces):
+        send("VW", M * r + a0, M * r + a1, [(cross, bits(off), "x%d" % c)])
+    for h in range(2):
+        need("p", [("s%d" % h, len(off))])
+        o = 1024 * far + 512 * h
+        hand("SW", o, o + 512, "fs", on)
+    send("VW", M * r, M * r + M, [(partner, bits(on), "vp")])
+    for c, (a0, a1) in enumerate(pieces):
+        need("p", [("x%d" % c, len(off))])
+        hand("VW", M * far + a0, M * far + a1, "fw", near)
+    hs, handed = 2 * len(on), n * len(near)
+
+    call("TA", ["pu"], ts, T.TA[:, 0:16], T.TI[:, 0:16], 15, None, AND)
+    call("MOD", ["TA"], ts, T.MOD[:], T.TA[:, 0:16], 0.0, None, OP.is_equal)
+    call("PB", ["pu"], ts, T.PB[:], T.TI[:, 0:1], 1, None, AND)
+    call("PC", ["PB"], ts, T.PC[:], T.PB[:], -4095.0, 4096.0, OP.mult, OP.add)
+    call("TM", ["pu"], ts, T.TA[:, 16:24], T.TI[:, 0:16:2], 15, None, AND)
+    call("MW", ["TM"], ts, T.MW[:], T.TA[:, 16:24], 1.0, None, OP.is_le)
+    call("ID", ["cp"], ts, T.ID[:], T.MI[:], 0.0, None, OP.is_equal)
+    call("IDN", ["ID"], ts, T.IDN[:], T.ID[:], -4096.0, None, OP.mult)
+    call("KZ", ["n0", "n1"], ts, T.K0[:], T.N0[:, 0:144], 0.0, None, OP.mult)
+    call("TS", ["p8"], ts, T.TS[:], T.T8[:], 4, None, SHR)
+    call("K0", ["KZ", "TS", "PC"], ts, T.K0[:, 15:143:16], T.TS[:], 0.0, T.PC[:], OP.is_equal, OP.mult)
+    call("E8", ["ei"], ts, T.E8L[:], T.EI[:], 0.0, None, OP.is_equal)
+    call("i6", ["ID"], copy, T.ID16[:], T.ID[:], AF.Copy, scale=16.0)
+    for u in range(16):
+        call("d%d" % u, ["ID", "MOD"], copy, T.DG[:, 128 * u:128 * u + 128], T.ID[:], AF.Copy, scale=T.MOD[:, u:u + 1])
+
+    call("tab", [("ltab", 32)], ts, T.PW[:, my], T.PW[:, my], -2048.0, None, OP.add)
+    for h in range(2):
+        o, c = T.HP[:, 512 * h:512 * h + 512], 1024 * h
+        call("pe%d" % h, ["ID", ("ls%d" % h, 16)], mm, o, T.ID[:], T.SEEN[:, c:c + 1024:2], True, False)
+        call("po%d" % h, ["i6", ("ls%d" % h, 16)], mm, o, T.ID16[:], T.SEEN[:, c + 1:c + 1024:2], False, True)
+        call("sw%d" % h, ["po%d" % h], copy, T.SW[:, 1024 * r + 512 * h:1024 * r + 512 * h + 512], o, AF.Copy)
+    call("cw", ["cb"], copy, T.CW[:], T.CB[:], AF.Copy, scale=0.5)
+    call("ra", [("lrk", 16)], ts, T.RKA[:], T.RKI[:, 4:8], 2048.0, None, OP.mult)
+    call("r0", [("lrk", 16), "cb"], tt, T.RT[:, 0:4], T.RKI[:, 0:4], T.CB[:], OP.add)
+    call("r1", ["ra", "cw"], tt, T.RT[:, 4:8], T.RKA[:], T.CW[:], OP.subtract)
+    call("r2", ["ra", "cw"], tt, T.RT[:, 8:11], T.CW[:, 1:4], T.RKA[:, 0:3], OP.subtract)
+    call("rt", ["E8", "r0", "r1", "r2"], mm, T.DD[:, 960:971], T.E8L[:], T.RT[:], True, True)
+
+    call("sf", [("lsd", 16)], cp, T.SF[:, 0:1], T.SDI[:])
+    call("si", [("lsd", 16)], ts, T.SI[:], T.SDI[:], 12, None, SHR)
+    call("sg", ["si"], ts, T.SF[:, 1:2], T.SI[:], 64.0, -262144.0, OP.mult, OP.add)
+    for h, w in enumerate(halves):
+        l64 = (T.VB[:, 0:96], T.HU[:, 256:352])[h]
+        i = lambda s: s + str(h)
+        call(i("s"), ["sf", i("n")], ts, T.L0[:, w], T.N0[:, w], T.SF[:, 0:1], None, OP.add)
+        call(i("l"), [i("s")], ts, T.L[:, w], T.L0[:, w], 4095, None, AND)
+        call(i("m"), [i("l")], ts, l64, T.L[:, w], 64.0, -262144.0, OP.mult, OP.add)
+        call(i("q"), [i("m")], copy, T.LL[:, w], l64, AF.Square, bias=4096.0, scale=1.0 / 64)
+        call(i("t"), [i("q"), "sg"], ts, T.TT[:, w], T.LL[:, w], T.SF[:, 1:2], None, OP.add)
+        call(i("b"), [i("t")], ts, T.B[:, w], T.TT[:, w], 6, 4095, SHR, AND)
+        call(i("c"), [i("b")], tt, T.BB[:, w], T.B[:, w], T.B[:, w], OP.mult)
+        call(i("a"), [i("c")], tt, T.AA[:, w], T.BB[:, w], l64, OP.add)
+    call("H", ["a0", "a1"], ts, T.H[:], T.AA[:, last], 15, 7, SHR, AND)
+    call("HH", ["H"], cp, T.H16[:], T.H[:])
+    call("LO", ["a0", "a1"], ts, T.LOW8[:], T.AA[:, last], 4, 255 << 3, SHR, AND)
+    call("EE", ["a0", "a1"], ts, T.EE[:], T.AA[:, last], 7, 2047, SHR, AND)
+    call("BH", ["b0", "b1"], ts, T.BH[:], T.B[:, last], -2048.0, None, OP.add)
+
+    Q8 = T.RQ[:, 0:48]
+    call("W", ["a0"], ts, T.W12[:], T.AA[:, 0:48], 4, 3 << 12, SHR, AND)
+    call("VV", ["W", "b0"], tt, T.VV[:], T.W12[:], T.B[:, 0:48], OP.add)
+    for w in range(7):
+        lim = T.DD[:, 960 + w:961 + w] if w < 4 else 4096.0 * (w - 3)
+        call("u%d" % w, ["VV", "rt"], ts, T.TM[:, blk(w)], T.VV[:], lim, T.DD[:, 964 + w:965 + w], OP.is_ge, OP.mult)
+        call("Q%d" % w, ["ID", "u%d" % w], mm, Q8, T.ID[:], T.TM[:, blk(w)], w == 0, w == 6)
+
+    D = [T.DD[:, 0:48], T.DD[:, 512:560], T.DD[:, 48:96]]
+    for i in range(3):
+        call("o%d" % i, ["Q6", "LO"], tt, T.S[:, blk(i)], T.LOW8[:, blk(i)], Q8, OP.add)
+        call("k%d" % i, ["HH", "MW"], copy, T.MK[:, pos(i)], T.MW[:].indirect(T.H16[:, blk(i)]), AF.Copy)
+        for c, (a, b) in enumerate(LOOKS[i]):
+            call("x%d%d" % (i, c), [("pk", 16), "tab", "k%d" % i, "E16"], tt, T.X1[:, pos(i, a, b)],
+                 T.PW[:].indirect(T.E16[:, 48 * i + a:48 * i + b]), T.MK[:, pos(i, a, b)], OP.mult)
+        done = ["x%d%d" % (i, c) for c in range(len(LOOKS[i]))]
+        for u in range(16):
+            call("y%d_%d" % (i, u), done + ["K0"] + (["M0"] if i == 2 else []), mm, D[i], T.K0[:, 15 - u:143 - u],
+                 T.X1[:, J * i + u:J * i + J:16], u == 0, False)
+        call("Y%d" % i, ["BH", "IDN"], mm, D[i], T.IDN[:], T.BH[:, blk(i)], False, True)
+    call("E16", ["o0", "o1", "o2"], ts, T.E16[:], T.S[:], 0.125, None, OP.mult)
+
+    for i in range(3):
+        c = lambda s: s + str(i)
+        call(c("M"), [c("Y"), "EE"], tt, T.M1[:, blk(i)], T.EE[:, blk(i)], D[i], OP.min)
+        call(c("C"), [c("M")], ts, T.C2[:, blk(i)], T.M1[:, blk(i)], 2046 if i < 2 else 2047, None, AND)
+        call(c("S"), [c("C"), "Q6"], tt, (T.S2 if i < 2 else T.G)[:, blk(i)], T.C2[:, blk(i)], Q8, OP.add)
+        if i < 2:
+            call(c("L"), [c("S")], ts, T.S16[:, blk(i)], T.S2[:, blk(i)], 0.5, None, OP.mult)
+            call(c("P"), [c("M")], ts, T.PAR[:, blk(i)], T.M1[:, blk(i)], 1, None, AND)
+            call(c("G"), [c("S"), c("P")], tt, T.G[:, blk(i)], T.S2[:, blk(i)], T.PAR[:, blk(i)], OP.add)
+            call(c("F"), [c("P")], ts, T.PP[:, blk(i)], T.PAR[:, blk(i)], float(-15 * (4096 >> (r + 4))), float(4096 >> r), OP.mult, OP.add)
+    seen = ["sw0", "sw1", ("sn", 2 * len(on)), ("s0", len(off)), ("s1", len(off)), ("fs", hs)]
+    call("h0", ["L0"] + seen, copy, T.X2[:, pos(0)], T.SW[:].indirect(T.S16[:, blk(0)]), AF.Copy)
+    call("ha", ["L1"] + seen, copy, T.X2[:, pos(1, HV)], T.SW[:].indirect(T.S16[:, 48 + HV:96]), AF.Copy)
+    call("hv", ["L1"] + seen, cp, T.X2[:, pos(1, 0, HV)], T.SW[:].indirect(T.S16[:, 48:48 + HV]))
+    for u in range(16):
+        call("z%d" % u, ["h0", "ha", "hv", "d%d" % u], mm, T.HU[:, two], T.DG[:, 128 * u:128 * u + 128], T.X2[:, u:2 * J:16], u == 0, u == 15)
+
+    E1, E2, T1, T2 = (T.HP[:, 64 * i:64 * i + 48] for i in range(4))
+    call("e1", ["G0", "G1", "sw0"], tt, E1, T.G[:, blk(1)], T.G[:, blk(0)], OP.subtract)
+    call("e2", ["S2", "G1", "sw0"], tt, E2, T.G[:, blk(2)], T.G[:, blk(1)], OP.subtract)
+    call("TK", ["z15", "F0", "F1"], tt, T.TK[:], T.HU[:, two], T.PP[:], OP.mult)
+    call("KB", ["TK"], ts, T.KB[:], T.TK[:], 12, 1, SHR, AND)
+    call("KK", ["KB"], tt, T.KK[:], T.KB[:, blk(0)], T.KB[:, blk(1)], OP.mult)
+    call("f1", ["KB", "e1"], tt, T1, T.KB[:, blk(0)], E1, OP.mult) if False else call("f1", ["KB", "e1"], tt, T.W[:], T.KB[:, blk(0)], E1, OP.mult)
+    call("f2", ["KK", "e2"], tt, T.KK[:], T.KK[:], E2, OP.mult)
+    call("f3", ["f1", "G0"], tt, T1, T.W[:], T.G[:, blk(0)], OP.add)
+    call("X", ["f2", "f3"], tt, T.X[:], T.KK[:], T1, OP.add)
+    call("X16", ["X"], cp, T.X16[:], T.X[:])
+
+    here = ["X16", ("lvec", 16), ("vp", len(on))] + [("x%d" % c, len(off)) for c in range(n)] + [("fw", handed)]
+    call("ya", here, copy, T.Y[:, 16 * YV:768], T.VW[:].indirect(T.X16[:, YV:48]), AF.Copy)
+    call("yv", here, cp, T.Y[:, 0:16 * YV], T.VW[:].indirect(T.X16[:, 0:YV]))
+
+    for q in "vat":
+        for name in ORDER[q].split():
+            deps, fn, args, kw = todo.pop(name)
+            need(q, deps)
+            fn(*args, **kw).then_inc(T.sem[q], 1)
+
+    need("s", ["X"])
+    g.sync.dma_start(T.chosen[:], T.X[:]).then_inc(T.sem.st, 16)
+    need("a", ["ya"])
+    act.dma_start(T.y[:, 16 * YV:768], T.Y[:, 16 * YV:768]).then_inc(T.sem.st, 16)
+    need("s", ["yv"])
+    g.sync.dma_start(T.y[:, 0:16 * YV], T.Y[:, 0:16 * YV]).then_inc(T.sem.st, 16)
+
+    need("p", [(q, len(ORDER[q].split())) for q in "vatp"])
+    sent = len(off) + len(on) + 2 * (len(off) + len(on)) + n * len(off) + len(on)
+    need("p", [("ls", sent), ("lf", hs + handed), ("vp", len(on)), ("fw", handed), ("fs", hs), ("pk", 16), ("sn", 2 * len(on)), ("st", 48)])
+    need("p", [("lsd", 16), ("ltab", 32), ("lrk", 16), ("ls0", 16), ("ls1", 16), ("lvec", 16)])

@@ -5,38 +5,45 @@ M, K, N = 2048, 48, 4
 J = 16 * K
 CUTS = (0, 896, 1536, 2048)
 YV = 24
-HV = 24
-LOOKS = (((0, 48),), ((0, 48),), ((0, 24), (24, 48)))
+HV = (8, 30)
+LOOKS = ((0, 36, 48), (0, 48), (0, 12, 20, 28, 36, 48))
+
+
+def run(s, n):
+    return " ".join(s % i for i in range(n))
+
+
 ORDER = {
-    "p": "pu n0 cp n1 ei cb p8",
-    "v": "TM TA PB sf ID MOD s0 tab s1 l0 si MW l1 m0 ra sg m1 E8 KZ r1 t0 r0 r2 t1 b0 b1 c0 c1 a0 a1 TS W H VV PC HH "
-         "u0 u1 u2 u3 u4 u5 u6 K0 LO o2 o1 o0 BH E16 IDN EE x00 x10 x20 M0 C0 S0 L0 P0 M1 x21 C1 F0 S1 L1 G0 hv P1 M2 C2 G1 S2 "
-         "e1 e2 F1 TK KB f1 KK f3 f2 X X16 yv",
-    "a": "d9 d14 d12 d1 d13 i6 cw d2 q0 q1 d11 d7 d0 d8 sw0 d15 sw1 k0 k1 k2 d3 d6 d4 d10 d5 h0 ha ya",
-    "t": " ".join(["pe0 po0 pe1 po1 rt"] + ["Q%d" % w for w in range(7)]
-                  + [" ".join(["y%d_%d" % (i, u) for u in range(16)] + ["Y%d" % i]) for i in range(3)] + ["z%d" % u for u in range(16)])}
+    "p": "cp n0 cb PF E8",
+    "v": "one KZ DZ TM TS ID PB MW sf si ph s0 s1 sg l0 l1 ra m0 m1 tab PC t0 r0 t1 b0 r1 b1 c0 c1 a0 K0 a1 r2 W EE LO VV HH LF "
+         "u0 u1 u2 u3 u4 u5 u6 pw E0 TA BH x00 E1 x01 x10 x20 M0 x21 C0 x22 S0 x23 L0 x24 M1 hv0 C1 MOD DO S1 DG L1 P hv1 "
+         "M2 F C2 D0 S2 TK0 e KB0 f1 g2 TK1 f3 KB1 sc X16 yv",
+    "a": "i6 DC IDN q0 q1 sw0 sw1 k0 k1 k2 ha0 ha1 X ya",
+    "t": " ".join(["pe0 po0 pe1 po1 rt"] + ["O%d " % i + run("Q%d_%%d" % i, 7) for i in range(3)] + [run("R0_%d", 7)]
+                  + [run("y0_%d", 16), "Y0", run("y1_%d", 16), "Y1", run("y2_%d", 16), "Y2", run("z0_%d", 16), run("z1_%d", 16)])}
 
 I4, F4, F2, H2, U2 = "int32", "float32", "bfloat16", "float16", "uint16"
 SCRATCH = {n: ("sbuf", [p, c], d) for n, p, c, d in (
-    ("PW", 128, 1024, I4), ("SW", 128, 4096, F2), ("VW", 128, 8192, F2), ("SEEN", 128, 2048, F2), ("SDI", 128, 1, I4),
-    ("RKI", 8, 8, I4), ("RKA", 8, 4, F4), ("RT", 8, 11, F4), ("TI", 128, 16, I4), ("TA", 128, 24, I4), ("T8", 128, 8, I4),
-    ("TS", 128, 8, I4), ("MI", 128, 128, F4), ("N0", 128, 192, I4), ("EI", 8, 128, F4), ("PB", 128, 1, I4),
-    ("PC", 128, 1, F4), ("K0", 128, 144, H2), ("ID", 128, 128, F2), ("ID16", 128, 128, F2), ("IDN", 128, 128, H2),
-    ("E8L", 8, 128, F4), ("MOD", 128, 16, F4), ("MW", 128, 8, F2), ("DG", 128, 2048, F2), ("SI", 128, 1, I4), ("SF", 128, 2, F4),
+    ("PW", 128, 1024, I4), ("PH", 128, 1024, U2), ("SW", 128, 4096, F2), ("VW", 128, 8192, F2), ("SEEN", 128, 2048, F2), ("SDI", 128, 1, I4),
+    ("RKI", 8, 8, I4), ("RKA", 8, 4, F4), ("RT", 8, 11, F4), ("TA", 128, 24, I4),
+    ("TS", 128, 8, I4), ("MI", 128, 128, I4), ("N0", 128, 96, I4), ("EI", 8, 128, F4), ("PB", 128, 1, I4),
+    ("PC", 128, 1, F4), ("K0", 128, 144, F2), ("ID", 128, 128, F2), ("ID16", 128, 128, F2), ("IDN", 128, 128, F2),
+    ("E8L", 8, 128, F4), ("MOD", 128, 16, F2), ("PF", 128, 1, F4), ("DO", 128, 2, U2), ("MW", 128, 8, F2), ("DG", 128, 2048, F2),
+    ("SI", 128, 1, I4), ("SF", 128, 2, F4),
     ("L0", 128, 192, I4), ("L", 128, 192, I4), ("LL", 128, 192, F4), ("TT", 128, 192, I4), ("B", 128, 192, I4),
-    ("BB", 128, 192, I4), ("AA", 128, 192, I4), ("H", 128, 144, I4), ("H16", 128, 144, U2), ("W12", 128, 48, I4),
-    ("VV", 128, 48, I4), ("TM", 128, 336, F2), ("CW", 8, 4, F4), ("CB", 8, 4, F4),
-    ("LOW8", 128, 144, I4), ("EE", 128, 144, I4), ("BH", 128, 144, H2),
-    ("S", 128, 144, I4), ("E16", 128, 144, U2), ("MK", 128, 2304, F2), ("X1", 128, 2304, H2), ("X2", 128, 1536, F2),
-    ("M1", 128, 144, I4), ("C2", 128, 144, I4), ("S2", 128, 144, I4), ("S16", 128, 96, U2), ("PAR", 128, 96, I4), ("G", 128, 144, I4),
-    ("PP", 128, 96, I4), ("TK", 128, 96, I4), ("KK", 128, 48, F4), ("KB", 128, 96, I4), ("X", 128, 48, F4), ("W", 128, 48, F4),
+    ("BB", 128, 192, I4), ("AA", 128, 192, I4), ("H16", 128, 144, U2), ("W12", 128, 48, I4),
+    ("VV", 128, 48, I4), ("TM", 128, 336, F2), ("CB", 8, 8, F4),
+    ("LOW8", 128, 144, I4), ("LOF", 128, 144, F2), ("EE", 128, 144, I4), ("BH", 128, 144, H2),
+    ("E16", 128, 144, U2), ("MK", 128, 2304, F2), ("X1", 128, 2304, H2), ("X2", 128, 1536, F2),
+    ("M1", 128, 144, I4), ("C2", 128, 144, I4), ("S16", 128, 96, U2), ("PAR", 128, 96, I4), ("G", 128, 144, I4),
+    ("PP", 128, 96, I4), ("TK", 128, 96, I4), ("D0", 128, 96, I4), ("D1", 128, 96, F4), ("SC", 128, 96, F4), ("KB", 128, 96, I4), ("X", 128, 48, F4), ("W", 128, 48, F4),
     ("X16", 128, 48, U2), ("Y", 128, 768, F2))}
 SCRATCH["HP"] = ("psum", [128, 1024], F4)
 SCRATCH["HU"] = ("psum", [128, 512], F4)
 SCRATCH["DD"] = ("psum", [128, 1024], F4)
 SCRATCH["RQ"] = ("psum", [128, 512], F4)
 SCRATCH["VB"] = ("psum", [128, 512], F4)
-SEMAPHORES = ["v", "a", "t", "p", "lsd", "ltab", "lrk", "ls0", "ls1", "lvec", "pk", "sn", "vp", "s0", "s1", "fs", "x0", "x1", "x2", "fw",
+SEMAPHORES = ["v", "a", "t", "p", "lsd", "ltab", "lrk", "ls0", "ls1", "lvec", "pk", "pn", "sn", "vp", "s0", "s1", "fs", "x0", "x1", "x2", "fw",
               "ls", "lf", "st"]
 
 
@@ -96,28 +103,29 @@ def rank_program(g, core, T, topo):
     def ramp(*args, **kw):
         g.iota(*args, **kw).then_inc(T.sem.p, 1)
 
-    def send(buf, a0, a1, dests):
+    def send(buf, a0, a1, dests, left="ls"):
         tr = []
         for d, mask, s in dests:
             rid, pid = topo.addr(d, core)
             tr.append(RemoteDMATransfer(dst_ids=[DstId(rid=rid, pnc=pid)], dma_engine_mask=mask, remote_sem=T.sem[s],
                                         srcs=[T[buf][:, a0:a1]], dsts=[T[buf][:, a0:a1]]))
-        g.remote_dma_fused(tr, local_sem=T.sem.ls)
+        g.remote_dma_fused(tr, local_sem=T.sem[left])
 
     def hand(buf, a0, a1, s, es):
         rid, pid = topo.addr(partner, core)
         g.remote_dma(T[buf][:, a0:a1], T[buf][:, a0:a1], T.sem[s], T.sem.lf, pid, rid, bits(es))
 
-    ramp(T.TI[:, 0:16], [[-1, 16]], 0, 1)
-    ramp(T.N0[:, 0:96], [[1597, 2], [6388, 48]], -(1 << 23), 0)
-    ramp(T.MI[:], [[1, 128]], 0, -1, **f)
-    ramp(T.N0[:, 96:192], [[1597, 2], [6388, 48]], 2 * 1597 - (1 << 23), 0)
-    ramp(T.EI[:], [[16, 8], [0, 16]], 0, -16, **f)
-    ramp(T.CB[:], [[4096, 4]], 0, 0, **f)
+    ramp(T.MI[:], [[1, 128]], 0, -1)
+    ramp(T.N0[:], [[1597, 2], [6388, 48]], -(1 << 23), 0)
+    ramp(T.CB[:], [[2048, 8]], 0, 0, **f)
+    ramp(T.PF[:], [[0, 1]], 0, 1, **f)
+    need("p", ["one"])
+    g.affine_select(T.E8L[:], T.EI[:], [[1, 8], [0, 16]], OP.is_equal, 0.0, 0, -1).then_inc(T.sem.p, 1)
     far = T.rank_of(cross)
+    need("p", ["ph"])
+    send("PH", 256 * r, 256 * r + 256, [(d, lanes[d], "pk") for d in (cross, diag)])
     need("p", ["tab"])
-    send("PW", 256 * r, 256 * r + 256, [(d, lanes[d], "pk") for d in (cross, diag, partner)])
-    ramp(T.T8[:], [[-16, 8]], 0, 1)
+    send("PW", 256 * r, 256 * r + 256, [(partner, lanes[partner], "pn")])
     for h in range(2):
         need("p", ["sw%d" % h])
         o = 1024 * r + 512 * h
@@ -126,44 +134,49 @@ def rank_program(g, core, T, topo):
     pieces = list(zip(CUTS, CUTS[1:]))
     n = len(pieces)
     for c, (a0, a1) in enumerate(pieces):
-        send("VW", M * r + a0, M * r + a1, [(cross, bits(off), "x%d" % c)])
+        send("VW", M * r + a0, M * r + a1, [(cross, bits(off), "x%d" % c)] + [(partner, bits(on), "vp")] * (c == 0))
     for h in range(2):
         need("p", [("s%d" % h, len(off))])
         o = 1024 * far + 512 * h
         hand("SW", o, o + 512, "fs", on)
-    send("VW", M * r, M * r + M, [(partner, bits(on), "vp")])
+    send("VW", M * r + CUTS[1], M * r + M, [(partner, bits(on), "vp")])
     for c, (a0, a1) in enumerate(pieces):
         need("p", [("x%d" % c, len(off))])
         hand("VW", M * far + a0, M * far + a1, "fw", near)
     hs, handed = 2 * len(on), n * len(near)
 
-    call("TA", ["pu"], ts, T.TA[:, 0:16], T.TI[:, 0:16], 15, None, AND)
+    call("TA", ["cp"], ts, T.TA[:, 0:16], T.MI[:, 0:16], 15, None, AND)
     call("MOD", ["TA"], ts, T.MOD[:], T.TA[:, 0:16], 0.0, None, OP.is_equal)
-    call("PB", ["pu"], ts, T.PB[:], T.TI[:, 0:1], 1, None, AND)
+    call("PB", ["cp"], ts, T.PB[:], T.MI[:, 0:1], 1, None, AND)
     call("PC", ["PB"], ts, T.PC[:], T.PB[:], -4095.0, 4096.0, OP.mult, OP.add)
-    call("TM", ["pu"], ts, T.TA[:, 16:24], T.TI[:, 0:16:2], 15, None, AND)
+    call("TM", ["cp"], ts, T.TA[:, 16:24], T.MI[:, 1:17:2], 15, None, AND)
     call("MW", ["TM"], ts, T.MW[:], T.TA[:, 16:24], 1.0, None, OP.is_le)
     call("ID", ["cp"], ts, T.ID[:], T.MI[:], 0.0, None, OP.is_equal)
-    call("IDN", ["ID"], ts, T.IDN[:], T.ID[:], -4096.0, None, OP.mult)
-    call("KZ", ["n0", "n1"], ts, T.K0[:], T.N0[:, 0:144], 0.0, None, OP.mult)
-    call("TS", ["p8"], ts, T.TS[:], T.T8[:], 4, None, SHR)
+    call("IDN", ["ID"], copy, T.IDN[:], T.ID[:], AF.Copy, scale=-4096.0)
+    call("KZ", [], vec.memset, T.K0[:], 0.0)
+    call("TS", ["cp"], ts, T.TS[:], T.MI[:, 15:128:16], 4, None, SHR)
     call("K0", ["KZ", "TS", "PC"], ts, T.K0[:, 15:143:16], T.TS[:], 0.0, T.PC[:], OP.is_equal, OP.mult)
-    call("E8", ["ei"], ts, T.E8L[:], T.EI[:], 0.0, None, OP.is_equal)
+    call("one", [], vec.memset, T.EI[:], 1.0)
     call("i6", ["ID"], copy, T.ID16[:], T.ID[:], AF.Copy, scale=16.0)
-    for u in range(16):
-        call("d%d" % u, ["ID", "MOD"], copy, T.DG[:, 128 * u:128 * u + 128], T.ID[:], AF.Copy, scale=T.MOD[:, u:u + 1])
+    call("DZ", [], vec.memset, T.DG[:, 0:1024], 0.0)
+    call("DC", ["DZ"], copy, T.DG[:, 1024:2048], T.DG[:, 0:1024], AF.Copy)
+    call("DO", ["TA", "PF"], ts, T.DO[:, 0:1], T.TA[:, 0:1], 128.0, T.PF[:], OP.mult, OP.add)
+    call("DG", ["DC", "DO", "MOD"], cp, T.DG[:].indirect(T.DO[:, 0:1]), T.MOD[:])
 
-    call("tab", [("ltab", 32)], ts, T.PW[:, my], T.PW[:, my], -2048.0, None, OP.add)
+    call("ph", [("ltab", 32)], cp, T.PH[:, my], T.PW[:, my])
+    call("tab", ["ph"], ts, T.PW[:, my], T.PW[:, my], -2048.0, None, OP.add)
+    lo = 256 * min(far, T.rank_of(diag))
+    assert abs(far - T.rank_of(diag)) == 1
+    call("pw", [("pk", len(off))], ts, T.PW[:, lo:lo + 512], T.PH[:, lo:lo + 512], -2048.0, None, OP.add)
     for h in range(2):
         o, c = T.HP[:, 512 * h:512 * h + 512], 1024 * h
         call("pe%d" % h, ["ID", ("ls%d" % h, 16)], mm, o, T.ID[:], T.SEEN[:, c:c + 1024:2], True, False)
         call("po%d" % h, ["i6", ("ls%d" % h, 16)], mm, o, T.ID16[:], T.SEEN[:, c + 1:c + 1024:2], False, True)
         call("sw%d" % h, ["po%d" % h], copy, T.SW[:, 1024 * r + 512 * h:1024 * r + 512 * h + 512], o, AF.Copy)
-    call("cw", ["cb"], copy, T.CW[:], T.CB[:], AF.Copy, scale=0.5)
     call("ra", [("lrk", 16)], ts, T.RKA[:], T.RKI[:, 4:8], 2048.0, None, OP.mult)
-    call("r0", [("lrk", 16), "cb"], tt, T.RT[:, 0:4], T.RKI[:, 0:4], T.CB[:], OP.add)
-    call("r1", ["ra", "cw"], tt, T.RT[:, 4:8], T.RKA[:], T.CW[:], OP.subtract)
-    call("r2", ["ra", "cw"], tt, T.RT[:, 8:11], T.CW[:, 1:4], T.RKA[:, 0:3], OP.subtract)
+    call("r0", [("lrk", 16), "cb"], tt, T.RT[:, 0:4], T.RKI[:, 0:4], T.CB[:, 0:8:2], OP.add)
+    call("r1", ["ra", "cb"], tt, T.RT[:, 4:8], T.RKA[:], T.CB[:, 0:4], OP.subtract)
+    call("r2", ["ra", "cb"], tt, T.RT[:, 8:11], T.CB[:, 1:4], T.RKA[:, 0:3], OP.subtract)
     call("rt", ["E8", "r0", "r1", "r2"], mm, T.DD[:, 960:971], T.E8L[:], T.RT[:], True, True)
 
     call("sf", [("lsd", 16)], cp, T.SF[:, 0:1], T.SDI[:])
@@ -172,7 +185,7 @@ def rank_program(g, core, T, topo):
     for h, w in enumerate(halves):
         l64 = (T.VB[:, 0:96], T.HU[:, 256:352])[h]
         i = lambda s: s + str(h)
-        call(i("s"), ["sf", i("n")], ts, T.L0[:, w], T.N0[:, w], T.SF[:, 0:1], None, OP.add)
+        call(i("s"), ["sf", "n0"], ts, T.L0[:, w], T.N0[:], T.SF[:, 0:1], 3194.0 * h, OP.add, OP.add)
         call(i("l"), [i("s")], ts, T.L[:, w], T.L0[:, w], 4095, None, AND)
         call(i("m"), [i("l")], ts, l64, T.L[:, w], 64.0, -262144.0, OP.mult, OP.add)
         call(i("q"), [i("m")], copy, T.LL[:, w], l64, AF.Square, bias=4096.0, scale=1.0 / 64)
@@ -180,64 +193,75 @@ def rank_program(g, core, T, topo):
         call(i("b"), [i("t")], ts, T.B[:, w], T.TT[:, w], 6, 4095, SHR, AND)
         call(i("c"), [i("b")], tt, T.BB[:, w], T.B[:, w], T.B[:, w], OP.mult)
         call(i("a"), [i("c")], tt, T.AA[:, w], T.BB[:, w], l64, OP.add)
-    call("H", ["a0", "a1"], ts, T.H[:], T.AA[:, last], 15, 7, SHR, AND)
-    call("HH", ["H"], cp, T.H16[:], T.H[:])
-    call("LO", ["a0", "a1"], ts, T.LOW8[:], T.AA[:, last], 4, 255 << 3, SHR, AND)
     call("EE", ["a0", "a1"], ts, T.EE[:], T.AA[:, last], 7, 2047, SHR, AND)
+    call("HH", ["EE"], ts, T.H16[:], T.EE[:], 1.0 / 256, -127.5 / 256, OP.mult, OP.add)
+    call("LO", ["a0", "a1"], ts, T.LOW8[:], T.AA[:, last], 4, 255 << 3, SHR, AND)
+    call("LF", ["LO"], cp, T.LOF[:], T.LOW8[:])
     call("BH", ["b0", "b1"], ts, T.BH[:], T.B[:, last], -2048.0, None, OP.add)
 
     Q8 = T.RQ[:, 0:48]
+    O = [T.VB[:, 256:304], T.HU[:, 0:48], T.HU[:, 48:96]]
     call("W", ["a0"], ts, T.W12[:], T.AA[:, 0:48], 4, 3 << 12, SHR, AND)
     call("VV", ["W", "b0"], tt, T.VV[:], T.W12[:], T.B[:, 0:48], OP.add)
+    for i in range(3):
+        call("O%d" % i, ["ID", "LF"], mm, O[i], T.ID[:], T.LOF[:, blk(i)], True, False)
     for w in range(7):
         lim = T.DD[:, 960 + w:961 + w] if w < 4 else 4096.0 * (w - 3)
         call("u%d" % w, ["VV", "rt"], ts, T.TM[:, blk(w)], T.VV[:], lim, T.DD[:, 964 + w:965 + w], OP.is_ge, OP.mult)
-        call("Q%d" % w, ["ID", "u%d" % w], mm, Q8, T.ID[:], T.TM[:, blk(w)], w == 0, w == 6)
+        for i in range(3):
+            call("Q%d_%d" % (i, w), ["u%d" % w], mm, O[i], T.ID[:], T.TM[:, blk(w)], False, w == 6)
+        for i in range(2):
+            call("R%d_%d" % (i, w), ["u6"], mm, T.RQ[:, blk(i)], T.ID[:], T.TM[:, blk(w)], w == 0, w == 6)
+    call("E0", ["Q0_6"], ts, T.E16[:, blk(0)], O[0], 0.125, None, OP.mult)
+    call("E1", ["Q2_6"], ts, T.E16[:, 48:144], T.HU[:, two], 0.125, None, OP.mult)
 
-    D = [T.DD[:, 0:48], T.DD[:, 512:560], T.DD[:, 48:96]]
+    merged = "M" in place
+    D = [T.DD[:, 0:48], T.DD[:, 48:96], T.DD[:, 512:560]] if merged else [T.DD[:, 0:48], T.DD[:, 512:560], T.DD[:, 48:96]]
     for i in range(3):
-        call("o%d" % i, ["Q6", "LO"], tt, T.S[:, blk(i)], T.LOW8[:, blk(i)], Q8, OP.add)
         call("k%d" % i, ["HH", "MW"], copy, T.MK[:, pos(i)], T.MW[:].indirect(T.H16[:, blk(i)]), AF.Copy)
-        for c, (a, b) in enumerate(LOOKS[i]):
-            call("x%d%d" % (i, c), [("pk", 16), "tab", "k%d" % i, "E16"], tt, T.X1[:, pos(i, a, b)],
+        cuts = LOOKS[i]
+        for c, (a, b) in enumerate(zip(cuts, cuts[1:])):
+            call("x%d%d" % (i, c), [("pn", len(on)), "pw", "tab", "k%d" % i, "E%d" % min(i, 1)], tt, T.X1[:, pos(i, a, b)],
                  T.PW[:].indirect(T.E16[:, 48 * i + a:48 * i + b]), T.MK[:, pos(i, a, b)], OP.mult)
-        done = ["x%d%d" % (i, c) for c in range(len(LOOKS[i]))]
+        done = ["x%d%d" % (i, c) for c in range(len(cuts) - 1)] + ["M0"] * (i == 2 and not merged)
         for u in range(16):
-            call("y%d_%d" % (i, u), done + ["K0"] + (["M0"] if i == 2 else []), mm, D[i], T.K0[:, 15 - u:143 - u],
-                 T.X1[:, J * i + u:J * i + J:16], u == 0, False)
+            call("y%d_%d" % (i, u), done + ["K0", "u6"], mm, D[i], T.K0[:, 15 - u:143 - u], T.X1[:, J * i + u:J * i + J:16], u == 0, False)
         call("Y%d" % i, ["BH", "IDN"], mm, D[i], T.IDN[:], T.BH[:, blk(i)], False, True)
-    call("E16", ["o0", "o1", "o2"], ts, T.E16[:], T.S[:], 0.125, None, OP.mult)
 
-    for i in range(3):
-        c = lambda s: s + str(i)
-        call(c("M"), [c("Y"), "EE"], tt, T.M1[:, blk(i)], T.EE[:, blk(i)], D[i], OP.min)
-        call(c("C"), [c("M")], ts, T.C2[:, blk(i)], T.M1[:, blk(i)], 2046 if i < 2 else 2047, None, AND)
-        call(c("S"), [c("C"), "Q6"], tt, (T.S2 if i < 2 else T.G)[:, blk(i)], T.C2[:, blk(i)], Q8, OP.add)
-        if i < 2:
-            call(c("L"), [c("S")], ts, T.S16[:, blk(i)], T.S2[:, blk(i)], 0.5, None, OP.mult)
-            call(c("P"), [c("M")], ts, T.PAR[:, blk(i)], T.M1[:, blk(i)], 1, None, AND)
-            call(c("G"), [c("S"), c("P")], tt, T.G[:, blk(i)], T.S2[:, blk(i)], T.PAR[:, blk(i)], OP.add)
-            call(c("F"), [c("P")], ts, T.PP[:, blk(i)], T.PAR[:, blk(i)], float(-15 * (4096 >> (r + 4))), float(4096 >> r), OP.mult, OP.add)
+    first = [("", two, T.DD[:, two], T.RQ[:, two])] if merged else [("0", blk(0), D[0], Q8), ("1", blk(1), D[1], Q8)]
+    for i, w, d, q in first + [("2", blk(2), D[2], Q8)]:
+        call("M" + i, ["Y" + (i or "1"), "EE"], tt, T.M1[:, w], T.EE[:, w], d, OP.min)
+        call("C" + i, ["M" + i], ts, T.C2[:, w], T.M1[:, w], 2047, None, AND)
+        call("S" + i, ["C" + i, "R0_6"] + ["R1_6"] * merged, tt, T.G[:, w], T.C2[:, w], q, OP.add)
+        if i != "2":
+            call("L" + i, ["S" + i], ts, T.S16[:, w], T.G[:, w], 0.5, -0.25, OP.mult, OP.add)
+    call("P", ["M"] if merged else ["M0", "M1"], ts, T.PAR[:], T.M1[:, two], 1, None, AND)
+    call("F", ["P"], ts, T.PP[:], T.PAR[:], float(-15 * (4096 >> (r + 4))), float(4096 >> r), OP.mult, OP.add)
     seen = ["sw0", "sw1", ("sn", 2 * len(on)), ("s0", len(off)), ("s1", len(off)), ("fs", hs)]
-    call("h0", ["L0"] + seen, copy, T.X2[:, pos(0)], T.SW[:].indirect(T.S16[:, blk(0)]), AF.Copy)
-    call("ha", ["L1"] + seen, copy, T.X2[:, pos(1, HV)], T.SW[:].indirect(T.S16[:, 48 + HV:96]), AF.Copy)
-    call("hv", ["L1"] + seen, cp, T.X2[:, pos(1, 0, HV)], T.SW[:].indirect(T.S16[:, 48:48 + HV]))
-    for u in range(16):
-        call("z%d" % u, ["h0", "ha", "hv", "d%d" % u], mm, T.HU[:, two], T.DG[:, 128 * u:128 * u + 128], T.X2[:, u:2 * J:16], u == 0, u == 15)
+    HU = (T.HU[:, 128:176], T.VB[:, 128:176])
+    for i in range(2):
+        L = ["L" if merged else "L%d" % i]
+        if HV[i]:
+            call("hv%d" % i, seen + L, cp, T.X2[:, pos(i, 0, HV[i])], T.SW[:].indirect(T.S16[:, 48 * i:48 * i + HV[i]]))
+        call("ha%d" % i, seen + L, copy, T.X2[:, pos(i, HV[i])], T.SW[:].indirect(T.S16[:, 48 * i + HV[i]:48 * i + 48]), AF.Copy)
+        for u in range(16):
+            d = 128 * (-u % 16)
+            call("z%d_%d" % (i, u), ["hv%d" % i] * (HV[i] > 0) + ["ha%d" % i, "DG", "E1"], mm, HU[i], T.DG[:, d:d + 128],
+                 T.X2[:, J * i + u:J * i + J:16], u == 0, u == 15)
+        call("TK%d" % i, ["z%d_15" % i, "F"], tt, T.TK[:, blk(i)], HU[i], T.PP[:, blk(i)], OP.mult)
+        call("KB%d" % i, ["TK%d" % i, "D0"], ts, (T.KB[:, blk(0)], T.D0[:, 1:96:2])[i], T.TK[:, blk(i)], 12, 1, SHR, AND)
 
-    E1, E2, T1, T2 = (T.HP[:, 64 * i:64 * i + 48] for i in range(4))
-    call("e1", ["G0", "G1", "sw0"], tt, E1, T.G[:, blk(1)], T.G[:, blk(0)], OP.subtract)
-    call("e2", ["S2", "G1", "sw0"], tt, E2, T.G[:, blk(2)], T.G[:, blk(1)], OP.subtract)
-    call("TK", ["z15", "F0", "F1"], tt, T.TK[:], T.HU[:, two], T.PP[:], OP.mult)
-    call("KB", ["TK"], ts, T.KB[:], T.TK[:], 12, 1, SHR, AND)
-    call("KK", ["KB"], tt, T.KK[:], T.KB[:, blk(0)], T.KB[:, blk(1)], OP.mult)
-    call("f1", ["KB", "e1"], tt, T1, T.KB[:, blk(0)], E1, OP.mult) if False else call("f1", ["KB", "e1"], tt, T.W[:], T.KB[:, blk(0)], E1, OP.mult)
-    call("f2", ["KK", "e2"], tt, T.KK[:], T.KK[:], E2, OP.mult)
-    call("f3", ["f1", "G0"], tt, T1, T.W[:], T.G[:, blk(0)], OP.add)
-    call("X", ["f2", "f3"], tt, T.X[:], T.KK[:], T1, OP.add)
-    call("X16", ["X"], cp, T.X16[:], T.X[:])
+    E, T1, T2 = T.HP[:, 0:96], T.HP[:, 128:176], T.HP[:, 192:240]
+    call("e", (["S"] if merged else ["S0", "S1"]) + ["S2", "sw0"], tt, E, T.G[:, 48:144], T.G[:, two], OP.subtract)
+    call("f1", ["KB0", "e"], tt, T.W[:], T.KB[:, blk(0)], T.HP[:, blk(0)], OP.mult)
+    call("g2", ["KB0", "e"], tt, T.D1[:, 0:96:2], T.KB[:, blk(0)], T.HP[:, blk(1)], OP.mult)
+    call("f3", ["f1"], tt, T.D1[:, 1:96:2], T.W[:], T.G[:, blk(0)], OP.add)
+    call("D0", [], vec.memset, T.D0[:], 0)
+    call("sc", ["KB1", "g2", "f3"], vec.tensor_tensor_scan, T.SC[:], T.D0[:], T.D1[:], 0.0, OP.mult, OP.add)
+    call("X", ["sc"], copy, T.X[:], T.SC[:, 1:96:2], AF.Copy)
+    call("X16", ["sc"], cp, T.X16[:], T.SC[:, 1:96:2])
 
-    here = ["X16", ("lvec", 16), ("vp", len(on))] + [("x%d" % c, len(off)) for c in range(n)] + [("fw", handed)]
+    here = ["X16", ("lvec", 16), ("vp", 2 * len(on))] + [("x%d" % c, len(off)) for c in range(n)] + [("fw", handed)]
     call("ya", here, copy, T.Y[:, 16 * YV:768], T.VW[:].indirect(T.X16[:, YV:48]), AF.Copy)
     call("yv", here, cp, T.Y[:, 0:16 * YV], T.VW[:].indirect(T.X16[:, 0:YV]))
 
@@ -255,6 +279,7 @@ def rank_program(g, core, T, topo):
     g.sync.dma_start(T.y[:, 0:16 * YV], T.Y[:, 0:16 * YV]).then_inc(T.sem.st, 16)
 
     need("p", [(q, len(ORDER[q].split())) for q in "vatp"])
-    sent = len(off) + len(on) + 2 * (len(off) + len(on)) + n * len(off) + len(on)
-    need("p", [("ls", sent), ("lf", hs + handed), ("vp", len(on)), ("fw", handed), ("fs", hs), ("pk", 16), ("sn", 2 * len(on)), ("st", 48)])
+    sent = len(off) + len(on) + 2 * (len(off) + len(on)) + n * len(off) + 2 * len(on)
+    need("p", [("ls", sent), ("lf", hs + handed), ("vp", 2 * len(on)), ("fw", handed), ("fs", hs), ("pk", len(off)), ("pn", len(on)),
+               ("sn", 2 * len(on)), ("st", 48)])
     need("p", [("lsd", 16), ("ltab", 32), ("lrk", 16), ("ls0", 16), ("ls1", 16), ("lvec", 16)])

from concourse.bass import DstId, RemoteDMATransfer
from concourse.mybir import AluOpType as OP, ActivationFunctionType as AF

M, K, N = 2048, 48, 4
J = 16 * K
CUTS = (0, 896, 1536, 2048)
YV = 24
HV = (8, 30)
LOOKS = ((0, 36, 48), (0, 48), (0, 12, 20, 28, 36, 48))


def run(s, n):
    return " ".join(s % i for i in range(n))


ORDER = {
    "p": "cp n0 cb PF E8",
    "v": "one KZ DZ TM TS ID PB MW sf si ph s0 s1 sg l0 l1 ra m0 m1 tab PC t0 r0 t1 b0 r1 b1 c0 c1 a0 K0 a1 r2 W EE LO VV HH LF "
         "u0 u1 u2 u3 u4 u5 u6 pw E0 TA BH x00 E1 x01 x10 x20 M0 x21 C0 x22 S0 x23 L0 x24 M1 hv0 C1 MOD DO S1 DG L1 P hv1 "
         "M2 F C2 D0 S2 TK0 e KB0 f1 g2 TK1 f3 KB1 sc X16 yv",
    "a": "i6 DC IDN q0 q1 sw0 sw1 k0 k1 k2 ha0 ha1 X ya",
    "t": " ".join(["pe0 po0 pe1 po1 rt"] + ["O%d " % i + run("Q%d_%%d" % i, 7) for i in range(3)] + [run("R0_%d", 7)]
                  + [run("y0_%d", 16), "Y0", run("y1_%d", 16), "Y1", run("y2_%d", 16), "Y2", run("z0_%d", 16), run("z1_%d", 16)])}

I4, F4, F2, H2, U2 = "int32", "float32", "bfloat16", "float16", "uint16"
SCRATCH = {n: ("sbuf", [p, c], d) for n, p, c, d in (
    ("PW", 128, 1024, I4), ("PH", 128, 1024, U2), ("SW", 128, 4096, F2), ("VW", 128, 8192, F2), ("SEEN", 128, 2048, F2), ("SDI", 128, 1, I4),
    ("RKI", 8, 8, I4), ("RKA", 8, 4, F4), ("RT", 8, 11, F4), ("TA", 128, 24, I4),
    ("TS", 128, 8, I4), ("MI", 128, 128, I4), ("N0", 128, 96, I4), ("EI", 8, 128, F4), ("PB", 128, 1, I4),
    ("PC", 128, 1, F4), ("K0", 128, 144, F2), ("ID", 128, 128, F2), ("ID16", 128, 128, F2), ("IDN", 128, 128, F2),
    ("E8L", 8, 128, F4), ("MOD", 128, 16, F2), ("PF", 128, 1, F4), ("DO", 128, 2, U2), ("MW", 128, 8, F2), ("DG", 128, 2048, F2),
    ("SI", 128, 1, I4), ("SF", 128, 2, F4),
    ("L0", 128, 192, I4), ("L", 128, 192, I4), ("LL", 128, 192, F4), ("TT", 128, 192, I4), ("B", 128, 192, I4),
    ("BB", 128, 192, I4), ("AA", 128, 192, I4), ("H16", 128, 144, U2), ("W12", 128, 48, I4),
    ("VV", 128, 48, I4), ("TM", 128, 336, F2), ("CB", 8, 8, F4),
    ("LOW8", 128, 144, I4), ("LOF", 128, 144, F2), ("EE", 128, 144, I4), ("BH", 128, 144, H2),
    ("E16", 128, 144, U2), ("MK", 128, 2304, F2), ("X1", 128, 2304, H2), ("X2", 128, 1536, F2),
    ("M1", 128, 144, I4), ("C2", 128, 144, I4), ("S16", 128, 96, U2), ("PAR", 128, 96, I4), ("G", 128, 144, I4),
    ("PP", 128, 96, I4), ("TK", 128, 96, I4), ("D0", 128, 96, I4), ("D1", 128, 96, F4), ("SC", 128, 96, F4), ("KB", 128, 96, I4), ("X", 128, 48, F4), ("W", 128, 48, F4),
    ("X16", 128, 48, U2), ("Y", 128, 768, F2))}
SCRATCH["HP"] = ("psum", [128, 1024], F4)
SCRATCH["HU"] = ("psum", [128, 512], F4)
SCRATCH["DD"] = ("psum", [128, 1024], F4)
SCRATCH["RQ"] = ("psum", [128, 512], F4)
SCRATCH["VB"] = ("psum", [128, 512], F4)
SEMAPHORES = ["v", "a", "t", "p", "lsd", "ltab", "lrk", "ls0", "ls1", "lvec", "pk", "pn", "sn", "vp", "s0", "s1", "fs", "x0", "x1", "x2", "fw",
              "ls", "lf", "st"]


def rank_program(g, core, T, topo):
    r = T.rank_of(core)
    if r is None:
        return
    others = [c for c in T.cores if c != core]
    partner = [c for c in others if c in topo.cores_of(core)][0]
    cross = [c for c in others if c != partner and topo.die(c) == topo.die(core)][0]
    diag = [c for c in others if c not in (partner, cross)][0]
    off = topo.engines(core, cross)
    near = topo.engines(core, partner)
    on = [e for e in near if e not in off]
    bits = lambda es: sum(1 << e for e in es)
    half = len(off) // 2
    lanes = {partner: bits(on), cross: bits(off[:half]), diag: bits(off[half:])}
    vec, act, pe = g.vector, g.scalar, g.tensor
    eng = {"v": vec, "a": act, "t": pe, "p": g, "s": g.sync}
    place = {name: (q, i + 1) for q in ORDER for i, name in enumerate(ORDER[q].split())}
    todo = {}
    lvl = {q: {} for q in eng}

    def need(q, deps):
        for d in deps:
            s, n = place[d] if d in place else d
            if lvl[q].get(s, 0) < n:
                eng[q].wait_ge(T.sem[s], n)
                lvl[q][s] = n

    def call(name, deps, f, *args, **kw):
        todo[name] = (deps, f, args, kw)

    def blk(i):
        return slice(48 * i, 48 * i + 48)

    def pos(i, a=0, b=48):
        return slice(J * i + 16 * a, J * i + 16 * b)

    ts, tt, cp, copy, mm = vec.tensor_scalar, vec.tensor_tensor, vec.tensor_copy, act.activation, pe.matmul
    SHR, AND = OP.arith_shift_right, OP.bitwise_and
    two, last = slice(0, 96), slice(48, 192)
    halves = (slice(0, 96), slice(96, 192))

    my = slice(256 * r, 256 * r + 256)
    g.sync.dma_start(T.SDI[:], T.sd[:]).then_inc(T.sem.lsd, 16)
    act.dma_start(T.PW[1:128:2, my], T.ali[:]).then_inc(T.sem.ltab, 16)
    g.sync.dma_start(T.PW[0:128:2, my], T.thr[:]).then_inc(T.sem.ltab, 16)
    act.dma_start(T.RKI[:], T.rk[:]).then_inc(T.sem.lrk, 16)
    for h in range(2):
        w = slice(1024 * h, 1024 * h + 1024)
        g.sync.dma_start(T.SEEN[:, w], T.seen[:, w]).then_inc(T.sem["ls%d" % h], 16)
    g.sync.dma_start(T.VW[:, M * r:M * r + M], T.vec[:]).then_inc(T.sem.lvec, 16)

    f = {"allow_small_or_imprecise_dtypes": True}

    def ramp(*args, **kw):
        g.iota(*args, **kw).then_inc(T.sem.p, 1)

    def send(buf, a0, a1, dests, left="ls"):
        tr = []
        for d, mask, s in dests:
            rid, pid = topo.addr(d, core)
            tr.append(RemoteDMATransfer(dst_ids=[DstId(rid=rid, pnc=pid)], dma_engine_mask=mask, remote_sem=T.sem[s],
                                        srcs=[T[buf][:, a0:a1]], dsts=[T[buf][:, a0:a1]]))
        g.remote_dma_fused(tr, local_sem=T.sem[left])

    def hand(buf, a0, a1, s, es):
        rid, pid = topo.addr(partner, core)
        g.remote_dma(T[buf][:, a0:a1], T[buf][:, a0:a1], T.sem[s], T.sem.lf, pid, rid, bits(es))

    ramp(T.MI[:], [[1, 128]], 0, -1)
    ramp(T.N0[:], [[1597, 2], [6388, 48]], -(1 << 23), 0)
    ramp(T.CB[:], [[2048, 8]], 0, 0, **f)
    ramp(T.PF[:], [[0, 1]], 0, 1, **f)
    need("p", ["one"])
    g.affine_select(T.E8L[:], T.EI[:], [[1, 8], [0, 16]], OP.is_equal, 0.0, 0, -1).then_inc(T.sem.p, 1)
    far = T.rank_of(cross)
    need("p", ["ph"])
    send("PH", 256 * r, 256 * r + 256, [(d, lanes[d], "pk") for d in (cross, diag)])
    need("p", ["tab"])
    send("PW", 256 * r, 256 * r + 256, [(partner, lanes[partner], "pn")])
    for h in range(2):
        need("p", ["sw%d" % h])
        o = 1024 * r + 512 * h
        send("SW", o, o + 512, [(cross, bits(off), "s%d" % h), (partner, bits(on), "sn")])
    need("p", [("lvec", 16)])
    pieces = list(zip(CUTS, CUTS[1:]))
    n = len(pieces)
    for c, (a0, a1) in enumerate(pieces):
        send("VW", M * r + a0, M * r + a1, [(cross, bits(off), "x%d" % c)] + [(partner, bits(on), "vp")] * (c == 0))
    for h in range(2):
        need("p", [("s%d" % h, len(off))])
        o = 1024 * far + 512 * h
        hand("SW", o, o + 512, "fs", on)
    send("VW", M * r + CUTS[1], M * r + M, [(partner, bits(on), "vp")])
    for c, (a0, a1) in enumerate(pieces):
        need("p", [("x%d" % c, len(off))])
        hand("VW", M * far + a0, M * far + a1, "fw", near)
    hs, handed = 2 * len(on), n * len(near)

    call("TA", ["cp"], ts, T.TA[:, 0:16], T.MI[:, 0:16], 15, None, AND)
    call("MOD", ["TA"], ts, T.MOD[:], T.TA[:, 0:16], 0.0, None, OP.is_equal)
    call("PB", ["cp"], ts, T.PB[:], T.MI[:, 0:1], 1, None, AND)
    call("PC", ["PB"], ts, T.PC[:], T.PB[:], -4095.0, 4096.0, OP.mult, OP.add)
    call("TM", ["cp"], ts, T.TA[:, 16:24], T.MI[:, 1:17:2], 15, None, AND)
    call("MW", ["TM"], ts, T.MW[:], T.TA[:, 16:24], 1.0, None, OP.is_le)
    call("ID", ["cp"], ts, T.ID[:], T.MI[:], 0.0, None, OP.is_equal)
    call("IDN", ["ID"], copy, T.IDN[:], T.ID[:], AF.Copy, scale=-4096.0)
    call("KZ", [], vec.memset, T.K0[:], 0.0)
    call("TS", ["cp"], ts, T.TS[:], T.MI[:, 15:128:16], 4, None, SHR)
    call("K0", ["KZ", "TS", "PC"], ts, T.K0[:, 15:143:16], T.TS[:], 0.0, T.PC[:], OP.is_equal, OP.mult)
    call("one", [], vec.memset, T.EI[:], 1.0)
    call("i6", ["ID"], copy, T.ID16[:], T.ID[:], AF.Copy, scale=16.0)
    call("DZ", [], vec.memset, T.DG[:, 0:1024], 0.0)
    call("DC", ["DZ"], copy, T.DG[:, 1024:2048], T.DG[:, 0:1024], AF.Copy)
    call("DO", ["TA", "PF"], ts, T.DO[:, 0:1], T.TA[:, 0:1], 128.0, T.PF[:], OP.mult, OP.add)
    call("DG", ["DC", "DO", "MOD"], cp, T.DG[:].indirect(T.DO[:, 0:1]), T.MOD[:])

    call("ph", [("ltab", 32)], cp, T.PH[:, my], T.PW[:, my])
    call("tab", ["ph"], ts, T.PW[:, my], T.PW[:, my], -2048.0, None, OP.add)
    lo = 256 * min(far, T.rank_of(diag))
    assert abs(far - T.rank_of(diag)) == 1
    call("pw", [("pk", len(off))], ts, T.PW[:, lo:lo + 512], T.PH[:, lo:lo + 512], -2048.0, None, OP.add)
    for h in range(2):
        o, c = T.HP[:, 512 * h:512 * h + 512], 1024 * h
        call("pe%d" % h, ["ID", ("ls%d" % h, 16)], mm, o, T.ID[:], T.SEEN[:, c:c + 1024:2], True, False)
        call("po%d" % h, ["i6", ("ls%d" % h, 16)], mm, o, T.ID16[:], T.SEEN[:, c + 1:c + 1024:2], False, True)
        call("sw%d" % h, ["po%d" % h], copy, T.SW[:, 1024 * r + 512 * h:1024 * r + 512 * h + 512], o, AF.Copy)
    call("ra", [("lrk", 16)], ts, T.RKA[:], T.RKI[:, 4:8], 2048.0, None, OP.mult)
    call("r0", [("lrk", 16), "cb"], tt, T.RT[:, 0:4], T.RKI[:, 0:4], T.CB[:, 0:8:2], OP.add)
    call("r1", ["ra", "cb"], tt, T.RT[:, 4:8], T.RKA[:], T.CB[:, 0:4], OP.subtract)
    call("r2", ["ra", "cb"], tt, T.RT[:, 8:11], T.CB[:, 1:4], T.RKA[:, 0:3], OP.subtract)
    call("rt", ["E8", "r0", "r1", "r2"], mm, T.DD[:, 960:971], T.E8L[:], T.RT[:], True, True)

    call("sf", [("lsd", 16)], cp, T.SF[:, 0:1], T.SDI[:])
    call("si", [("lsd", 16)], ts, T.SI[:], T.SDI[:], 12, None, SHR)
    call("sg", ["si"], ts, T.SF[:, 1:2], T.SI[:], 64.0, -262144.0, OP.mult, OP.add)
    for h, w in enumerate(halves):
        l64 = (T.VB[:, 0:96], T.HU[:, 256:352])[h]
        i = lambda s: s + str(h)
        call(i("s"), ["sf", "n0"], ts, T.L0[:, w], T.N0[:], T.SF[:, 0:1], 3194.0 * h, OP.add, OP.add)
        call(i("l"), [i("s")], ts, T.L[:, w], T.L0[:, w], 4095, None, AND)
        call(i("m"), [i("l")], ts, l64, T.L[:, w], 64.0, -262144.0, OP.mult, OP.add)
        call(i("q"), [i("m")], copy, T.LL[:, w], l64, AF.Square, bias=4096.0, scale=1.0 / 64)
        call(i("t"), [i("q"), "sg"], ts, T.TT[:, w], T.LL[:, w], T.SF[:, 1:2], None, OP.add)
        call(i("b"), [i("t")], ts, T.B[:, w], T.TT[:, w], 6, 4095, SHR, AND)
        call(i("c"), [i("b")], tt, T.BB[:, w], T.B[:, w], T.B[:, w], OP.mult)
        call(i("a"), [i("c")], tt, T.AA[:, w], T.BB[:, w], l64, OP.add)
    call("EE", ["a0", "a1"], ts, T.EE[:], T.AA[:, last], 7, 2047, SHR, AND)
    call("HH", ["EE"], ts, T.H16[:], T.EE[:], 1.0 / 256, -127.5 / 256, OP.mult, OP.add)
    call("LO", ["a0", "a1"], ts, T.LOW8[:], T.AA[:, last], 4, 255 << 3, SHR, AND)
    call("LF", ["LO"], cp, T.LOF[:], T.LOW8[:])
    call("BH", ["b0", "b1"], ts, T.BH[:], T.B[:, last], -2048.0, None, OP.add)

    Q8 = T.RQ[:, 0:48]
    O = [T.VB[:, 256:304], T.HU[:, 0:48], T.HU[:, 48:96]]
    call("W", ["a0"], ts, T.W12[:], T.AA[:, 0:48], 4, 3 << 12, SHR, AND)
    call("VV", ["W", "b0"], tt, T.VV[:], T.W12[:], T.B[:, 0:48], OP.add)
    for i in range(3):
        call("O%d" % i, ["ID", "LF"], mm, O[i], T.ID[:], T.LOF[:, blk(i)], True, False)
    for w in range(7):
        lim = T.DD[:, 960 + w:961 + w] if w < 4 else 4096.0 * (w - 3)
        call("u%d" % w, ["VV", "rt"], ts, T.TM[:, blk(w)], T.VV[:], lim, T.DD[:, 964 + w:965 + w], OP.is_ge, OP.mult)
        for i in range(3):
            call("Q%d_%d" % (i, w), ["u%d" % w], mm, O[i], T.ID[:], T.TM[:, blk(w)], False, w == 6)
        for i in range(2):
            call("R%d_%d" % (i, w), ["u6"], mm, T.RQ[:, blk(i)], T.ID[:], T.TM[:, blk(w)], w == 0, w == 6)
    call("E0", ["Q0_6"], ts, T.E16[:, blk(0)], O[0], 0.125, None, OP.mult)
    call("E1", ["Q2_6"], ts, T.E16[:, 48:144], T.HU[:, two], 0.125, None, OP.mult)

    merged = "M" in place
    D = [T.DD[:, 0:48], T.DD[:, 48:96], T.DD[:, 512:560]] if merged else [T.DD[:, 0:48], T.DD[:, 512:560], T.DD[:, 48:96]]
    for i in range(3):
        call("k%d" % i, ["HH", "MW"], copy, T.MK[:, pos(i)], T.MW[:].indirect(T.H16[:, blk(i)]), AF.Copy)
        cuts = LOOKS[i]
        for c, (a, b) in enumerate(zip(cuts, cuts[1:])):
            call("x%d%d" % (i, c), [("pn", len(on)), "pw", "tab", "k%d" % i, "E%d" % min(i, 1)], tt, T.X1[:, pos(i, a, b)],
                 T.PW[:].indirect(T.E16[:, 48 * i + a:48 * i + b]), T.MK[:, pos(i, a, b)], OP.mult)
        done = ["x%d%d" % (i, c) for c in range(len(cuts) - 1)] + ["M0"] * (i == 2 and not merged)
        for u in range(16):
            call("y%d_%d" % (i, u), done + ["K0", "u6"], mm, D[i], T.K0[:, 15 - u:143 - u], T.X1[:, J * i + u:J * i + J:16], u == 0, False)
        call("Y%d" % i, ["BH", "IDN"], mm, D[i], T.IDN[:], T.BH[:, blk(i)], False, True)

    first = [("", two, T.DD[:, two], T.RQ[:, two])] if merged else [("0", blk(0), D[0], Q8), ("1", blk(1), D[1], Q8)]
    for i, w, d, q in first + [("2", blk(2), D[2], Q8)]:
        call("M" + i, ["Y" + (i or "1"), "EE"], tt, T.M1[:, w], T.EE[:, w], d, OP.min)
        call("C" + i, ["M" + i], ts, T.C2[:, w], T.M1[:, w], 2047, None, AND)
        call("S" + i, ["C" + i, "R0_6"] + ["R1_6"] * merged, tt, T.G[:, w], T.C2[:, w], q, OP.add)
        if i != "2":
            call("L" + i, ["S" + i], ts, T.S16[:, w], T.G[:, w], 0.5, -0.25, OP.mult, OP.add)
    call("P", ["M"] if merged else ["M0", "M1"], ts, T.PAR[:], T.M1[:, two], 1, None, AND)
    call("F", ["P"], ts, T.PP[:], T.PAR[:], float(-15 * (4096 >> (r + 4))), float(4096 >> r), OP.mult, OP.add)
    seen = ["sw0", "sw1", ("sn", 2 * len(on)), ("s0", len(off)), ("s1", len(off)), ("fs", hs)]
    HU = (T.HU[:, 128:176], T.VB[:, 128:176])
    for i in range(2):
        L = ["L" if merged else "L%d" % i]
        if HV[i]:
            call("hv%d" % i, seen + L, cp, T.X2[:, pos(i, 0, HV[i])], T.SW[:].indirect(T.S16[:, 48 * i:48 * i + HV[i]]))
        call("ha%d" % i, seen + L, copy, T.X2[:, pos(i, HV[i])], T.SW[:].indirect(T.S16[:, 48 * i + HV[i]:48 * i + 48]), AF.Copy)
        for u in range(16):
            d = 128 * (-u % 16)
            call("z%d_%d" % (i, u), ["hv%d" % i] * (HV[i] > 0) + ["ha%d" % i, "DG", "E1"], mm, HU[i], T.DG[:, d:d + 128],
                 T.X2[:, J * i + u:J * i + J:16], u == 0, u == 15)
        call("TK%d" % i, ["z%d_15" % i, "F"], tt, T.TK[:, blk(i)], HU[i], T.PP[:, blk(i)], OP.mult)
        call("KB%d" % i, ["TK%d" % i, "D0"], ts, (T.KB[:, blk(0)], T.D0[:, 1:96:2])[i], T.TK[:, blk(i)], 12, 1, SHR, AND)

    E, T1, T2 = T.HP[:, 0:96], T.HP[:, 128:176], T.HP[:, 192:240]
    call("e", (["S"] if merged else ["S0", "S1"]) + ["S2", "sw0"], tt, E, T.G[:, 48:144], T.G[:, two], OP.subtract)
    call("f1", ["KB0", "e"], tt, T.W[:], T.KB[:, blk(0)], T.HP[:, blk(0)], OP.mult)
    call("g2", ["KB0", "e"], tt, T.D1[:, 0:96:2], T.KB[:, blk(0)], T.HP[:, blk(1)], OP.mult)
    call("f3", ["f1"], tt, T.D1[:, 1:96:2], T.W[:], T.G[:, blk(0)], OP.add)
    call("D0", [], vec.memset, T.D0[:], 0)
    call("sc", ["KB1", "g2", "f3"], vec.tensor_tensor_scan, T.SC[:], T.D0[:], T.D1[:], 0.0, OP.mult, OP.add)
    call("X", ["sc"], copy, T.X[:], T.SC[:, 1:96:2], AF.Copy)
    call("X16", ["sc"], cp, T.X16[:], T.SC[:, 1:96:2])

    here = ["X16", ("lvec", 16), ("vp", 2 * len(on))] + [("x%d" % c, len(off)) for c in range(n)] + [("fw", handed)]
    call("ya", here, copy, T.Y[:, 16 * YV:768], T.VW[:].indirect(T.X16[:, YV:48]), AF.Copy)
    call("yv", here, cp, T.Y[:, 0:16 * YV], T.VW[:].indirect(T.X16[:, 0:YV]))

    for q in "vat":
        for name in ORDER[q].split():
            deps, fn, args, kw = todo.pop(name)
            need(q, deps)
            fn(*args, **kw).then_inc(T.sem[q], 1)

    need("s", ["X"])
    g.sync.dma_start(T.chosen[:], T.X[:]).then_inc(T.sem.st, 16)
    need("a", ["ya"])
    act.dma_start(T.y[:, 16 * YV:768], T.Y[:, 16 * YV:768]).then_inc(T.sem.st, 16)
    need("s", ["yv"])
    g.sync.dma_start(T.y[:, 0:16 * YV], T.Y[:, 0:16 * YV]).then_inc(T.sem.st, 16)

    need("p", [(q, len(ORDER[q].split())) for q in "vatp"])
    sent = len(off) + len(on) + 2 * (len(off) + len(on)) + n * len(off) + 2 * len(on)
    need("p", [("ls", sent), ("lf", hs + handed), ("vp", 2 * len(on)), ("fw", handed), ("fs", hs), ("pk", len(off)), ("pn", len(on)),
               ("sn", 2 * len(on)), ("st", 48)])
    need("p", [("lsd", 16), ("ltab", 32), ("lrk", 16), ("ls0", 16), ("ls1", 16), ("lvec", 16)])
